import numpy as np
import ml_dtypes


def mxq(x, axis, fmt="e4m3"):
    dtype, down = {"e4m3": (ml_dtypes.float8_e4m3fn, 7), "e5m2": (ml_dtypes.float8_e5m2, 14)}[fmt]
    v = np.moveaxis(np.asarray(x, np.float32).astype(ml_dtypes.bfloat16).astype(np.float64), axis, -1)
    blocks = v.reshape(v.shape[:-1] + (-1, 32))
    amax = np.abs(blocks).max(-1, keepdims=True)
    byte = np.maximum(np.where(amax > 0, np.frexp(amax)[1] - 1 + 127, 0) - down, 1)
    scale = np.exp2(byte - 127.0)
    codes = (blocks / scale).astype(np.float32).astype(dtype).astype(np.float64)
    return np.moveaxis((codes * scale).reshape(v.shape), -1, axis)


WIDE = False


def mx_kscale(k):
    if not WIDE:
        return np.ones(k)
    levels = np.array([10, -10, 5, -5, 0])
    if k % 512:
        return np.exp2(np.random.permutation(np.resize(levels, k // 32))).repeat(32)
    a = np.empty((k // 512, 16))
    for p in range(k // 512):
        a[p, :8] = np.random.permutation(np.resize(levels, 8))
        for g in range(8):
            far = levels[np.abs(levels - a[p, g]) >= 10]
            a[p, g + 8] = far[np.random.randint(len(far))]
    return np.exp2(a.ravel()).repeat(32)


def f64(x):
    return np.asarray(x).astype(np.float64)


def striped(idx):
    return np.tile(idx.reshape(-1, 16).T, (8, 1)).astype(np.uint16)


def unstriped(offs):
    return offs[:16].T.reshape(-1).astype(np.int64)


def striped8(idx):
    return np.concatenate([x.reshape(-1, 16).T for x in idx]).astype(np.uint16)


def runs(offs, k):
    lists = np.stack([offs[16 * r : 16 * r + 16].T.reshape(-1) for r in range(8)]).astype(np.int64)
    return lists[np.arange(k) % 512 // 64]


def pack_weight(w):
    k, n = w.shape
    w = f64(np.asarray(w, np.float32).astype(ml_dtypes.bfloat16)).reshape(k // 32, 32, n)
    amax = np.abs(w).max(1)
    byte = np.clip(np.where(amax > 0, np.frexp(amax)[1] - 1 + 127 - 7, 1), 1, 254)
    scaled = (w * np.exp2(127.0 - byte)[:, None, :]).reshape(k, n).astype(np.float32)
    words = np.ascontiguousarray(scaled.reshape(k // 512, 128, 4, n).transpose(0, 1, 3, 2)).astype(ml_dtypes.float8_e4m3fn).view(np.uint8)
    return words, np.ascontiguousarray(byte.astype(np.uint8).reshape(k // 512, 16, n))


def unpack_weight(words, scales):
    g, p, n, _ = words.shape
    vals = np.ascontiguousarray(words).view(ml_dtypes.float8_e4m3fn).astype(np.float64) * np.repeat(np.exp2(scales.astype(np.float64) - 127.0), 8, axis=1)[..., None]
    return vals.transpose(0, 1, 3, 2).reshape(g * 512, n)


def sigmoid(v):
    return 1.0 / (1.0 + np.exp(-np.maximum(v, -700.0)))


K, T, S, N, H = 512, 2048, 512, 512, 512


def setup_inputs():
    n = np.random.standard_normal
    s = mx_kscale(K)[:, None]
    u = mx_kscale(H)
    packed_xT = pack_weight(n((K, T)) * s)
    return {
        "x_words": packed_xT[0],
        "x_scales": packed_xT[1],
        "w1": (n((K, H)) / np.sqrt(K) / s).astype(np.float32),
        "w2": (n((K, H)) / np.sqrt(K) / s).astype(np.float32),
        "gn": (np.random.uniform(0.5, 1.5, (H, 1)) * u[:, None]).astype(np.float32),
        "w3": (n((H, N)) / np.sqrt(H) / u[:, None]).astype(np.float32),
        "res": (2 * n((N, S))).astype(np.float32),
        "offs": striped(np.random.permutation(T)[:S]),
        "two": striped(np.random.permutation(T)[:S]),
        "nb": striped8(np.stack([np.random.permutation(S) for _ in range(8)])),
    }


def reference(x_words, x_scales, w1, w2, gn, w3, res, offs, two, nb):
    x_two = unpack_weight(x_words, x_scales)[:, unstriped(two)]
    c = sigmoid(mxq(f64(w2), 0, "e4m3").T @ x_two)
    cn = c[np.arange(H)[:, None], runs(nb, H)]
    xq = unpack_weight(x_words, x_scales)[:, unstriped(offs)]
    y = mxq(f64(w1), 0, "e4m3").T @ xq
    z = f64(gn) * (((4.0 * (c * cn)) / (c + cn)) * (y[np.arange(H)[:, None], runs(nb, H)] - y))
    return f64(res) + (mxq(f64(w3), 0, "e4m3").T @ mxq(z, 0, "e4m3"))

@@ -1,0 +1,167 @@
+from contextlib import ExitStack
+
+import concourse.mybir as mybir
+
+K, T, S, N, H = 512, 2048, 512, 512, 512
+FLOPS = 3 * 2 * 512 * 512 * 512
+
+F32 = mybir.dt.float32
+BF16 = mybir.dt.bfloat16
+I32 = mybir.dt.int32
+U32 = mybir.dt.uint32
+U16 = mybir.dt.uint16
+U8 = mybir.dt.uint8
+FP8X4 = mybir.dt.float8_e4m3fn_x4
+ACT = mybir.ActivationFunctionType
+ALU = mybir.AluOpType
+
+P = 128
+PACK = 4
+HALF = S // 2
+QUART = S // 4
+
+
+def tile_picked_harmflux_none_p_kernel(tc, x_words, x_scales, w1, w2, gn, w3, res, offs, two, nb, out):
+    nc = tc.nc
+    with ExitStack() as ctx:
+        keep = ctx.enter_context(tc.tile_pool(name="keep", bufs=1))
+        psum = ctx.enter_context(tc.psum_pool(name="psum", bufs=1))
+
+        def sb(name, shape, dtype):
+            return keep.tile(shape, dtype, name=name, align_bytes=64)
+
+        two_l = sb("two_l", [P, S // 16], U16)
+        offs_l = sb("offs_l", [P, S // 16], U16)
+        nb_l = sb("nb_l", [P, S // 16], U16)
+        xw = sb("xw", [P, T], U32)
+        xs = sb("xs", [P, T], U8)
+        nc.gpsimd.memset(xs[:].bitcast(I32), 0)
+        nc.sync.dma_start(two_l[:], two)
+        nc.sync.dma_start(offs_l[:], offs)
+        for q in range(4):
+            nc.sync.dma_start(xs[32 * q : 32 * q + 4, :].bitcast(I32), x_scales[0, 4 * q : 4 * q + 4, :].bitcast(I32))
+        nc.sync.dma_start(xw[:].bitcast(I32), x_words[0].rearrange("p n t -> p (n t)").bitcast(I32))
+
+        def load_halves(name, w):
+            halves = []
+            for h in range(2):
+                raw = sb(name + str(h), [P, PACK, HALF], F32)
+                nc.sync.dma_start(raw[:], w[:, h * HALF : (h + 1) * HALF].rearrange("(p j) c -> p j c", j=PACK))
+                halves.append(raw)
+            return halves
+
+        w2_raw = load_halves("w2_raw", w2)
+        w1_raw = load_halves("w1_raw", w1)
+        nc.sync.dma_start(nb_l[:], nb)
+        gain = sb("gain", [P, PACK], F32)
+        nc.sync.dma_start(gain[:], gn.rearrange("(p t) o -> p (t o)", t=PACK))
+        w3_raw = sb("w3_raw", [P, PACK, N], F32)
+        nc.sync.dma_start(w3_raw[:], w3.rearrange("(p j) c -> p j c", j=PACK))
+        res_sb = sb("res_sb", [P, 4, S], F32)
+        nc.sync.dma_start(res_sb[:], res.rearrange("(b p) j -> p b j", p=P))
+
+        def pick(name, lst):
+            sc = sb(name + "_s", [P, S], U8)
+            nc.vector.tensor_copy(sc[:], xs[:].indirect(lst[:]))
+            return sc
+
+        def pickw(name, lst):
+            wd = sb(name + "_w", [P, S], U32)
+            nc.vector.tensor_copy(wd[:], xw[:].indirect(lst[:]))
+            return wd
+
+        two_s = pick("two", two_l)
+        offs_s = pick("offs", offs_l)
+        two_w = pickw("two", two_l)
+        offs_w = pickw("offs", offs_l)
+
+        def dealt_cast(copy, dst, raw, h):
+            m = HALF // PACK
+            copy(
+                dst[:, :, h * m : (h + 1) * m, :].rearrange("p t m j -> p m t j"),
+                raw[:].rearrange("p j (m t) -> p m t j", t=PACK),
+            )
+
+        def quant(name, src, width):
+            codes = sb(name + "_c", [P, width], U32)
+            scales = sb(name + "_q", [P, width], U8)
+            nc.vector.quantize_mx(out=codes[:].bitcast(FP8X4), scales=scales[:], in_=src)
+            return codes, scales
+
+        def mm(o, wq, cols, xc, xsc):
+            nc.tensor.matmul_mx(out=o, lhsT=wq[0][:, cols].bitcast(FP8X4), lhsT_scale=wq[1][:, cols],
+                                rhs=xc.bitcast(FP8X4), rhs_scale=xsc, start=True, stop=True)
+
+        w2_bf = sb("w2_bf", [P, PACK, P, PACK], BF16)
+        dealt_cast(nc.scalar.copy, w2_bf, w2_raw[0], 0)
+        dealt_cast(nc.vector.tensor_copy, w2_bf, w2_raw[1], 1)
+        e = []
+        for t in range(PACK):
+            wq = quant("w2q%d" % t, w2_bf[:, t].rearrange("p m j -> p (m j)"), P)
+            acc = psum.tile([P, S], F32, name="bank%d" % t)
+            mm(acc[:], wq, slice(0, P), two_w[:], two_s[:])
+            et = sb("e%d" % t, [P, S], F32)
+            nc.scalar.activation(et[:], acc[:], ACT.Exp, scale=-1.0)
+            e.append(et)
+
+        w1_bf = sb("w1_bf", [P, PACK, P, PACK], BF16)
+        dealt_cast(nc.vector.tensor_copy, w1_bf, w1_raw[0], 0)
+        dealt_cast(nc.vector.tensor_copy, w1_bf, w1_raw[1], 1)
+        w1q = quant("w1q", w1_bf[:].rearrange("p t m j -> p (t m j)"), H)
+        y = []
+        for t in range(PACK):
+            acc = psum.tile([P, S], F32, name="bank%d" % (4 + t))
+            mm(acc[:], w1q, slice(t * P, (t + 1) * P), offs_w[:], offs_s[:])
+            yt = sb("y%d" % t, [P, S], F32)
+            nc.scalar.activation(yt[:], acc[:], ACT.Copy, scale=gain[:, t : t + 1])
+            y.append(yt)
+
+        sums, diffs, roots = [], [], []
+        for h in range(2):
+            cols = slice(h * HALF, (h + 1) * HALF)
+            lst = nb_l[:, h * HALF // 16 : (h + 1) * HALF // 16]
+            sm = sb("sum%d" % h, [P, PACK, HALF], F32)
+            for t in range(PACK):
+                nc.vector.tensor_copy(sm[:, t, :], e[t][:].indirect(lst))
+            for t in range(PACK):
+                nc.vector.tensor_tensor(sm[:, t, :], sm[:, t, :], e[t][:, cols], ALU.add)
+            sums.append(sm)
+
+        w3_bf = sb("w3_bf", [P, N, PACK], BF16)
+        nc.vector.tensor_copy(
+            w3_bf[:].rearrange("p (c i) j -> p c j i", i=4), w3_raw[:].rearrange("p j (c i) -> p c j i", i=4)
+        )
+        w3q = quant("w3q", w3_bf[:].rearrange("p c j -> p (c j)"), N)
+
+        for h in range(2):
+            cols = slice(h * HALF, (h + 1) * HALF)
+            lst = nb_l[:, h * HALF // 16 : (h + 1) * HALF // 16]
+            df = sb("diff%d" % h, [P, PACK, HALF], F32)
+            for t in range(PACK):
+                nc.scalar.activation(df[:, t, :], y[t][:].indirect(lst), ACT.Copy)
+            rts = []
+            for u in range(2):
+                rt = sb("root%d" % (2 * h + u), [P, PACK, QUART], F32)
+                nc.scalar.activation(rt[:], sums[h][:, :, u * QUART : (u + 1) * QUART], ACT.Abs_reciprocal_sqrt, scale=0.25, bias=0.5)
+                nc.scalar.activation(rt[:], rt[:], ACT.Square)
+                rts.append(rt)
+            for t in range(PACK):
+                nc.vector.tensor_tensor(df[:, t, :], df[:, t, :], y[t][:, cols], ALU.subtract)
+            for u in range(2):
+                q = 2 * h + u
+                sub = slice(u * QUART, (u + 1) * QUART)
+                z = sb("z%d" % q, [P, QUART, PACK], BF16)
+                nc.vector.tensor_tensor(
+                    z[:].rearrange("p (c i) t -> p c t i", i=4),
+                    df[:, :, sub].rearrange("p t (c i) -> p c t i", i=4),
+                    rts[u][:].rearrange("p t (c i) -> p c t i", i=4),
+                    ALU.mult,
+                )
+                zq = quant("zq%d" % q, z[:].rearrange("p c t -> p (c t)"), QUART)
+                acc = psum.tile([P, 4, QUART], F32, name="bank%d" % q)
+                for b in range(4):
+                    mm(acc[:, b, :], w3q, slice(b * P, (b + 1) * P), zq[0][:], zq[1][:])
+                o = sb("o%d" % q, [P, 4, QUART], F32)
+                jc = slice(q * QUART, (q + 1) * QUART)
+                nc.vector.tensor_tensor(o[:], acc[:], res_sb[:, :, jc], ALU.add)
+                nc.sync.dma_start(out[:, jc].rearrange("(b p) j -> p b j", p=P), o[:])

@@ -1,8 +1,9 @@
 from contextlib import ExitStack
 
 import concourse.mybir as mybir
+from concourse.masks import make_identity
 
-K, T, S, N, H = 512, 2048, 512, 512, 512
+T, S, H, N = 2048, 512, 512, 512
 FLOPS = 3 * 2 * 512 * 512 * 512
 
 F32 = mybir.dt.float32
@@ -18,7 +19,10 @@ ALU = mybir.AluOpType
 P = 128
 PACK = 4
 HALF = S // 2
-QUART = S // 4
+QUARTER = S // 4
+ROW_BLOCKS = N // P
+PER_COLUMN = 16
+SCALAR_E_GATHERS = 2
 
 
 def tile_picked_harmflux_none_p_kernel(tc, x_words, x_scales, w1, w2, gn, w3, res, offs, two, nb, out):
@@ -27,141 +31,208 @@ def tile_picked_harmflux_none_p_kernel(tc, x_words, x_scales, w1, w2, gn, w3, re
         keep = ctx.enter_context(tc.tile_pool(name="keep", bufs=1))
         psum = ctx.enter_context(tc.psum_pool(name="psum", bufs=1))
 
-        def sb(name, shape, dtype):
+        def sbuf(name, shape, dtype):
             return keep.tile(shape, dtype, name=name, align_bytes=64)
 
-        two_l = sb("two_l", [P, S // 16], U16)
-        offs_l = sb("offs_l", [P, S // 16], U16)
-        nb_l = sb("nb_l", [P, S // 16], U16)
-        xw = sb("xw", [P, T], U32)
-        xs = sb("xs", [P, T], U8)
-        nc.gpsimd.memset(xs[:].bitcast(I32), 0)
-        nc.sync.dma_start(two_l[:], two)
-        nc.sync.dma_start(offs_l[:], offs)
-        for q in range(4):
-            nc.sync.dma_start(xs[32 * q : 32 * q + 4, :].bitcast(I32), x_scales[0, 4 * q : 4 * q + 4, :].bitcast(I32))
-        nc.sync.dma_start(xw[:].bitcast(I32), x_words[0].rearrange("p n t -> p (n t)").bitcast(I32))
+        def bank(number, shape):
+            return psum.tile(shape, F32, name="bank%d" % number)
 
-        def load_halves(name, w):
-            halves = []
-            for h in range(2):
-                raw = sb(name + str(h), [P, PACK, HALF], F32)
-                nc.sync.dma_start(raw[:], w[:, h * HALF : (h + 1) * HALF].rearrange("(p j) c -> p j c", j=PACK))
-                halves.append(raw)
-            return halves
+        two_list = sbuf("two_list", [P, S // PER_COLUMN], U16)
+        offs_list = sbuf("offs_list", [P, S // PER_COLUMN], U16)
+        nb_list = sbuf("nb_list", [P, S // PER_COLUMN], U16)
+        table_words = sbuf("table_words", [P, T], U32)
+        table_scales = sbuf("table_scales", [P, T], U8)
+        nc.gpsimd.memset(table_scales[:].bitcast(I32), 0)
+        nc.sync.dma_start(two_list[:], two)
+        nc.sync.dma_start(offs_list[:], offs)
+        for quadrant in range(4):
+            nc.sync.dma_start(
+                table_scales[32 * quadrant : 32 * quadrant + 4, :].bitcast(I32),
+                x_scales[0, 4 * quadrant : 4 * quadrant + 4, :].bitcast(I32),
+            )
+        nc.sync.dma_start(table_words[:].bitcast(I32), x_words[0].rearrange("p n s -> p (n s)").bitcast(I32))
 
-        w2_raw = load_halves("w2_raw", w2)
-        w1_raw = load_halves("w1_raw", w1)
-        nc.sync.dma_start(nb_l[:], nb)
-        gain = sb("gain", [P, PACK], F32)
+        def load_weight(name, w):
+            raw = sbuf(name, [P, PACK, w.shape[1]], F32)
+            nc.sync.dma_start(raw[:], w.rearrange("(p s) c -> p s c", s=PACK))
+            return raw
+
+        w2_raw = load_weight("w2_raw", w2)
+        w1_halves = [load_weight("w1_raw%d" % half, w1[:, half * H // 2 : (half + 1) * H // 2]) for half in range(2)]
+        nc.sync.dma_start(nb_list[:], nb)
+        gain = sbuf("gain", [P, PACK], F32)
         nc.sync.dma_start(gain[:], gn.rearrange("(p t) o -> p (t o)", t=PACK))
-        w3_raw = sb("w3_raw", [P, PACK, N], F32)
-        nc.sync.dma_start(w3_raw[:], w3.rearrange("(p j) c -> p j c", j=PACK))
-        res_sb = sb("res_sb", [P, 4, S], F32)
-        nc.sync.dma_start(res_sb[:], res.rearrange("(b p) j -> p b j", p=P))
+        w3_raw = load_weight("w3_raw", w3)
+        res_rows = sbuf("res_rows", [P, ROW_BLOCKS, S], F32)
+        nc.sync.dma_start(res_rows[:], res.rearrange("(b p) j -> p b j", p=P))
 
-        def pick(name, lst):
-            sc = sb(name + "_s", [P, S], U8)
-            nc.vector.tensor_copy(sc[:], xs[:].indirect(lst[:]))
-            return sc
+        identity = sbuf("identity", [P, P], F32)
+        make_identity(nc, identity[:])
+        minus_gain = sbuf("minus_gain", [P, PACK], F32)
+        nc.gpsimd.tensor_scalar(minus_gain[:], gain[:], -1.0, 0.0, ALU.mult, ALU.add)
 
-        def pickw(name, lst):
-            wd = sb(name + "_w", [P, S], U32)
-            nc.vector.tensor_copy(wd[:], xw[:].indirect(lst[:]))
-            return wd
+        def pick(name, table, entries, dtype):
+            picked = sbuf(name, [P, S], dtype)
+            nc.vector.tensor_copy(picked[:], table[:].indirect(entries[:]))
+            return picked
 
-        two_s = pick("two", two_l)
-        offs_s = pick("offs", offs_l)
-        two_w = pickw("two", two_l)
-        offs_w = pickw("offs", offs_l)
+        two_scales = pick("two_scales", table_scales, two_list, U8)
+        offs_scales = pick("offs_scales", table_scales, offs_list, U8)
+        two_words = pick("two_words", table_words, two_list, U32)
+        offs_words = pick("offs_words", table_words, offs_list, U32)
 
-        def dealt_cast(copy, dst, raw, h):
-            m = HALF // PACK
-            copy(
-                dst[:, :, h * m : (h + 1) * m, :].rearrange("p t m j -> p m t j"),
-                raw[:].rearrange("p j (m t) -> p m t j", t=PACK),
+        def round_and_deal(copy, target, source):
+            copy(target.rearrange("p t m s -> p m t s"), source.rearrange("p s m t -> p m t s"))
+
+        def quantize(name, values, width):
+            words = sbuf(name + "_words", [P, width], U32)
+            scales = sbuf(name + "_scales", [P, width], U8)
+            nc.vector.quantize_mx(out=words[:].bitcast(FP8X4), scales=scales[:], in_=values)
+            return words, scales
+
+        def product(acc, weight, block, moving):
+            cols = slice(block * P, (block + 1) * P)
+            nc.tensor.matmul_mx(
+                out=acc,
+                lhsT=weight[0][:, cols].bitcast(FP8X4),
+                lhsT_scale=weight[1][:, cols],
+                rhs=moving[0][:].bitcast(FP8X4),
+                rhs_scale=moving[1][:],
+                start=True,
+                stop=True,
             )
 
-        def quant(name, src, width):
-            codes = sb(name + "_c", [P, width], U32)
-            scales = sb(name + "_q", [P, width], U8)
-            nc.vector.quantize_mx(out=codes[:].bitcast(FP8X4), scales=scales[:], in_=src)
-            return codes, scales
-
-        def mm(o, wq, cols, xc, xsc):
-            nc.tensor.matmul_mx(out=o, lhsT=wq[0][:, cols].bitcast(FP8X4), lhsT_scale=wq[1][:, cols],
-                                rhs=xc.bitcast(FP8X4), rhs_scale=xsc, start=True, stop=True)
-
-        w2_bf = sb("w2_bf", [P, PACK, P, PACK], BF16)
-        dealt_cast(nc.scalar.copy, w2_bf, w2_raw[0], 0)
-        dealt_cast(nc.vector.tensor_copy, w2_bf, w2_raw[1], 1)
+        w2_columns = w2_raw[:].rearrange("p s (m t) -> p s m t", t=PACK)
+        w2_dealt = [sbuf("w2_dealt%d" % pair, [P, 2, P, PACK], BF16) for pair in range(2)]
+        round_and_deal(nc.vector.tensor_copy, w2_dealt[0][:], w2_columns[:, :, :, :2])
+        round_and_deal(nc.scalar.copy, w2_dealt[1][:], w2_columns[:, :, :, 2:])
+        w1_dealt = sbuf("w1_dealt", [P, PACK, P, PACK], BF16)
+        w1_columns = [raw[:].rearrange("p s (m t) -> p s m t", t=PACK) for raw in w1_halves]
+        round_and_deal(nc.scalar.copy, w1_dealt[:, :, : P // 2, :], w1_columns[0])
         e = []
         for t in range(PACK):
-            wq = quant("w2q%d" % t, w2_bf[:, t].rearrange("p m j -> p (m j)"), P)
-            acc = psum.tile([P, S], F32, name="bank%d" % t)
-            mm(acc[:], wq, slice(0, P), two_w[:], two_s[:])
-            et = sb("e%d" % t, [P, S], F32)
-            nc.scalar.activation(et[:], acc[:], ACT.Exp, scale=-1.0)
-            e.append(et)
+            w2_mx = quantize("w2_%d" % t, w2_dealt[t // 2][:, t % 2].rearrange("p m s -> p (m s)"), P)
+            acc = bank(t, [P, S])
+            product(acc[:], w2_mx, 0, (two_words, two_scales))
+            e.append(sbuf("e%d" % t, [P, S], F32))
+            nc.scalar.activation(e[t][:], acc[:], ACT.Exp, scale=-1.0)
 
-        w1_bf = sb("w1_bf", [P, PACK, P, PACK], BF16)
-        dealt_cast(nc.vector.tensor_copy, w1_bf, w1_raw[0], 0)
-        dealt_cast(nc.vector.tensor_copy, w1_bf, w1_raw[1], 1)
-        w1q = quant("w1q", w1_bf[:].rearrange("p t m j -> p (t m j)"), H)
-        y = []
+        round_and_deal(nc.vector.tensor_copy, w1_dealt[:, :, P // 2 :, :], w1_columns[1])
+        w1_mx = quantize("w1", w1_dealt[:].rearrange("p t m s -> p (t m s)"), H)
+        minus_y = []
         for t in range(PACK):
-            acc = psum.tile([P, S], F32, name="bank%d" % (4 + t))
-            mm(acc[:], w1q, slice(t * P, (t + 1) * P), offs_w[:], offs_s[:])
-            yt = sb("y%d" % t, [P, S], F32)
-            nc.scalar.activation(yt[:], acc[:], ACT.Copy, scale=gain[:, t : t + 1])
-            y.append(yt)
+            acc = bank(4 + t, [P, S])
+            product(acc[:], w1_mx, t, (offs_words, offs_scales))
+            minus_y.append(sbuf("minus_y%d" % t, [P, S], F32))
+            nc.scalar.activation(minus_y[t][:], acc[:], ACT.Copy, scale=minus_gain[:, t : t + 1])
 
-        sums, diffs, roots = [], [], []
-        for h in range(2):
-            cols = slice(h * HALF, (h + 1) * HALF)
-            lst = nb_l[:, h * HALF // 16 : (h + 1) * HALF // 16]
-            sm = sb("sum%d" % h, [P, PACK, HALF], F32)
-            for t in range(PACK):
-                nc.vector.tensor_copy(sm[:, t, :], e[t][:].indirect(lst))
-            for t in range(PACK):
-                nc.vector.tensor_tensor(sm[:, t, :], sm[:, t, :], e[t][:, cols], ALU.add)
-            sums.append(sm)
+        def neighbours(half):
+            return nb_list[:, half * HALF // PER_COLUMN : (half + 1) * HALF // PER_COLUMN]
 
-        w3_bf = sb("w3_bf", [P, N, PACK], BF16)
-        nc.vector.tensor_copy(
-            w3_bf[:].rearrange("p (c i) j -> p c j i", i=4), w3_raw[:].rearrange("p j (c i) -> p c j i", i=4)
-        )
-        w3q = quant("w3q", w3_bf[:].rearrange("p c j -> p (c j)"), N)
-
-        for h in range(2):
-            cols = slice(h * HALF, (h + 1) * HALF)
-            lst = nb_l[:, h * HALF // 16 : (h + 1) * HALF // 16]
-            df = sb("diff%d" % h, [P, PACK, HALF], F32)
+        def turn(acc, tiles, first_place, start, stop):
             for t in range(PACK):
-                nc.scalar.activation(df[:, t, :], y[t][:].indirect(lst), ACT.Copy)
-            rts = []
-            for u in range(2):
-                rt = sb("root%d" % (2 * h + u), [P, PACK, QUART], F32)
-                nc.scalar.activation(rt[:], sums[h][:, :, u * QUART : (u + 1) * QUART], ACT.Abs_reciprocal_sqrt, scale=0.25, bias=0.5)
-                nc.scalar.activation(rt[:], rt[:], ACT.Square)
-                rts.append(rt)
-            for t in range(PACK):
-                nc.vector.tensor_tensor(df[:, t, :], df[:, t, :], y[t][:, cols], ALU.subtract)
-            for u in range(2):
-                q = 2 * h + u
-                sub = slice(u * QUART, (u + 1) * QUART)
-                z = sb("z%d" % q, [P, QUART, PACK], BF16)
-                nc.vector.tensor_tensor(
-                    z[:].rearrange("p (c i) t -> p c t i", i=4),
-                    df[:, :, sub].rearrange("p t (c i) -> p c t i", i=4),
-                    rts[u][:].rearrange("p t (c i) -> p c t i", i=4),
-                    ALU.mult,
+                nc.tensor.matmul(
+                    acc[:, t * P : (t + 1) * P],
+                    tiles[t][:, first_place : first_place + QUARTER],
+                    identity[:],
+                    start=start and t == 0,
+                    stop=stop and t == PACK - 1,
+                    is_transpose=True,
                 )
-                zq = quant("zq%d" % q, z[:].rearrange("p c t -> p (c t)"), QUART)
-                acc = psum.tile([P, 4, QUART], F32, name="bank%d" % q)
-                for b in range(4):
-                    mm(acc[:, b, :], w3q, slice(b * P, (b + 1) * P), zq[0][:], zq[1][:])
-                o = sb("o%d" % q, [P, 4, QUART], F32)
-                jc = slice(q * QUART, (q + 1) * QUART)
-                nc.vector.tensor_tensor(o[:], acc[:], res_sb[:, :, jc], ALU.add)
-                nc.sync.dma_start(out[:, jc].rearrange("(b p) j -> p b j", p=P), o[:])
+
+        e_sum = [bank(quarter, [P, H]) for quarter in range(4)]
+        y_diff = [bank(4 + quarter, [P, H]) for quarter in range(4)]
+
+        def open_sums(banks, tiles, half):
+            for quarter in (2 * half, 2 * half + 1):
+                turn(banks[quarter], tiles, quarter * QUARTER, True, False)
+
+        def close_sums(banks, near, half):
+            for u in range(2):
+                turn(banks[2 * half + u], [near[:, t, :] for t in range(PACK)], u * QUARTER, False, True)
+
+        def add_e_near(half, on_scalar):
+            near = sbuf("e_near%d" % half, [P, PACK, HALF], F32)
+            for t in range(PACK):
+                if t < on_scalar:
+                    nc.scalar.activation(near[:, t, :], e[t][:].indirect(neighbours(half)), ACT.Copy)
+                else:
+                    nc.vector.tensor_copy(near[:, t, :], e[t][:].indirect(neighbours(half)))
+            close_sums(e_sum, near, half)
+
+        def add_y_near(half):
+            near = sbuf("y_near%d" % half, [P, PACK, HALF], F32)
+            for t in range(PACK):
+                looked_up = minus_y[t][:].indirect(neighbours(half))
+                nc.vector.tensor_scalar(near[:, t, :], looked_up, -1.0, 0.0, ALU.mult, ALU.add)
+            close_sums(y_diff, near, half)
+
+        open_sums(e_sum, e, 0)
+        add_e_near(0, 0)
+        open_sums(e_sum, e, 1)
+        add_e_near(1, SCALAR_E_GATHERS)
+        open_sums(y_diff, minus_y, 0)
+        add_y_near(0)
+        open_sums(y_diff, minus_y, 1)
+
+        w3_rounded = sbuf("w3_rounded", [P, N, PACK], BF16)
+        nc.gpsimd.tensor_scalar(
+            w3_rounded[:].rearrange("p (c i) s -> p c s i", i=4),
+            w3_raw[:].rearrange("p s (c i) -> p c s i", i=4),
+            1.0,
+            0.0,
+            ALU.mult,
+            ALU.add,
+        )
+        w3_mx = quantize("w3", w3_rounded[:].rearrange("p c s -> p (c s)"), N)
+
+        def in_pairs(acc):
+            return acc[:].rearrange("j (u v p) -> j u p v", u=2, v=2)
+
+        def factor(quarter):
+            root = sbuf("factor%d" % quarter, [P, 2, P, 2], F32)
+            nc.scalar.activation(root[:], in_pairs(e_sum[quarter]), ACT.Abs_reciprocal_sqrt, scale=0.25, bias=0.5)
+            nc.scalar.activation(root[:], root[:], ACT.Square)
+            return root
+
+        def flux(quarter, root):
+            turned = sbuf("z_turned%d" % quarter, [P, 2, P, 2], BF16)
+            nc.vector.tensor_tensor(turned[:], in_pairs(y_diff[quarter]), root[:], ALU.mult)
+            pairs = turned[:].rearrange("j u p v -> j (u p v)").bitcast(F32)
+            back = bank(quarter, [P, 2, QUARTER])
+            for u in range(2):
+                nc.tensor.transpose(back[:, u, :], pairs[:, u * P : (u + 1) * P], identity[:])
+            z = sbuf("z%d" % quarter, [P, QUARTER * PACK], BF16)
+            nc.scalar.copy(z[:].bitcast(F32).rearrange("p (j u) -> p j u", u=2), back[:].rearrange("p u j -> p j u"))
+            return z
+
+        def layer(quarter, z):
+            z_mx = quantize("z%d" % quarter, z[:], QUARTER)
+            acc = bank(4 + quarter, [P, ROW_BLOCKS, QUARTER])
+            for block in range(ROW_BLOCKS):
+                product(acc[:, block, :], w3_mx, block, z_mx)
+            return acc
+
+        def finish(quarter, acc, pieces):
+            places = slice(quarter * QUARTER, (quarter + 1) * QUARTER)
+            rows = out[:, places].rearrange("(b p) j -> p b j", p=P)
+            step = ROW_BLOCKS // pieces
+            for first in range(0, ROW_BLOCKS, step):
+                blocks = slice(first, first + step)
+                result = sbuf("result%d_%d" % (quarter, first), [P, step, QUARTER], F32)
+                nc.vector.tensor_tensor(result[:], acc[:, blocks, :], res_rows[:, blocks, places], ALU.add)
+                nc.sync.dma_start(rows[:, blocks, :], result[:])
+
+        roots = [factor(0), factor(1)]
+        z = [flux(0, roots[0]), flux(1, roots[1])]
+        add_y_near(1)
+        roots.extend([factor(2), factor(3)])
+        sums = [layer(0, z[0])]
+        z.append(flux(2, roots[2]))
+        sums.append(layer(1, z[1]))
+        z.append(flux(3, roots[3]))
+        for quarter in (2, 3):
+            finish(quarter - 2, sums[quarter - 2], 1)
+            sums.append(layer(quarter, z[quarter]))
+        finish(2, sums[2], 1)
+        finish(3, sums[3], 2)

@@ -22,7 +22,7 @@ HALF = S // 2
 QUARTER = S // 4
 ROW_BLOCKS = N // P
 PER_COLUMN = 16
-SCALAR_E_GATHERS = 2
+SCALAR_E_GATHERS = 3
 
 
 def tile_picked_harmflux_none_p_kernel(tc, x_words, x_scales, w1, w2, gn, w3, res, offs, two, nb, out):
@@ -69,7 +69,7 @@ def tile_picked_harmflux_none_p_kernel(tc, x_words, x_scales, w1, w2, gn, w3, re
         identity = sbuf("identity", [P, P], F32)
         make_identity(nc, identity[:])
         minus_gain = sbuf("minus_gain", [P, PACK], F32)
-        nc.gpsimd.tensor_scalar(minus_gain[:], gain[:], -1.0, 0.0, ALU.mult, ALU.add)
+        nc.vector.tensor_scalar_mul(minus_gain[:], gain[:], -1.0)
 
         def pick(name, table, entries, dtype):
             picked = sbuf(name, [P, S], dtype)
@@ -167,22 +167,18 @@ def tile_picked_harmflux_none_p_kernel(tc, x_words, x_scales, w1, w2, gn, w3, re
                 nc.vector.tensor_scalar(near[:, t, :], looked_up, -1.0, 0.0, ALU.mult, ALU.add)
             close_sums(y_diff, near, half)
 
-        open_sums(e_sum, e, 0)
+        for half in range(2):
+            open_sums(e_sum, e, half)
         add_e_near(0, 0)
-        open_sums(e_sum, e, 1)
         add_e_near(1, SCALAR_E_GATHERS)
-        open_sums(y_diff, minus_y, 0)
+        for half in range(2):
+            open_sums(y_diff, minus_y, half)
         add_y_near(0)
-        open_sums(y_diff, minus_y, 1)
 
         w3_rounded = sbuf("w3_rounded", [P, N, PACK], BF16)
-        nc.gpsimd.tensor_scalar(
+        nc.vector.tensor_copy(
             w3_rounded[:].rearrange("p (c i) s -> p c s i", i=4),
             w3_raw[:].rearrange("p s (c i) -> p c s i", i=4),
-            1.0,
-            0.0,
-            ALU.mult,
-            ALU.add,
         )
         w3_mx = quantize("w3", w3_rounded[:].rearrange("p c s -> p (c s)"), N)
 
@@ -224,15 +220,14 @@ def tile_picked_harmflux_none_p_kernel(tc, x_words, x_scales, w1, w2, gn, w3, re
                 nc.sync.dma_start(rows[:, blocks, :], result[:])
 
         roots = [factor(0), factor(1)]
-        z = [flux(0, roots[0]), flux(1, roots[1])]
         add_y_near(1)
-        roots.extend([factor(2), factor(3)])
-        sums = [layer(0, z[0])]
-        z.append(flux(2, roots[2]))
-        sums.append(layer(1, z[1]))
-        z.append(flux(3, roots[3]))
-        for quarter in (2, 3):
-            finish(quarter - 2, sums[quarter - 2], 1)
-            sums.append(layer(quarter, z[quarter]))
-        finish(2, sums[2], 1)
-        finish(3, sums[3], 2)
+        z, sums = [], []
+        for step in range(6):
+            if step < 2:
+                roots.append(factor(step + 2))
+            if step < 4:
+                z.append(flux(step, roots[step]))
+            if 1 <= step < 5:
+                sums.append(layer(step - 1, z[step - 1]))
+            if step >= 2:
+                finish(step - 2, sums[step - 2], 2 if step == 5 else 1)

from contextlib import ExitStack

import concourse.mybir as mybir
from concourse.masks import make_identity

T, S, H, N = 2048, 512, 512, 512
FLOPS = 3 * 2 * 512 * 512 * 512

F32 = mybir.dt.float32
BF16 = mybir.dt.bfloat16
I32 = mybir.dt.int32
U32 = mybir.dt.uint32
U16 = mybir.dt.uint16
U8 = mybir.dt.uint8
FP8X4 = mybir.dt.float8_e4m3fn_x4
ACT = mybir.ActivationFunctionType
ALU = mybir.AluOpType

P = 128
PACK = 4
HALF = S // 2
QUARTER = S // 4
ROW_BLOCKS = N // P
PER_COLUMN = 16
SCALAR_E_GATHERS = 3


def tile_picked_harmflux_none_p_kernel(tc, x_words, x_scales, w1, w2, gn, w3, res, offs, two, nb, out):
    nc = tc.nc
    with ExitStack() as ctx:
        keep = ctx.enter_context(tc.tile_pool(name="keep", bufs=1))
        psum = ctx.enter_context(tc.psum_pool(name="psum", bufs=1))

        def sbuf(name, shape, dtype):
            return keep.tile(shape, dtype, name=name, align_bytes=64)

        def bank(number, shape):
            return psum.tile(shape, F32, name="bank%d" % number)

        two_list = sbuf("two_list", [P, S // PER_COLUMN], U16)
        offs_list = sbuf("offs_list", [P, S // PER_COLUMN], U16)
        nb_list = sbuf("nb_list", [P, S // PER_COLUMN], U16)
        table_words = sbuf("table_words", [P, T], U32)
        table_scales = sbuf("table_scales", [P, T], U8)
        nc.gpsimd.memset(table_scales[:].bitcast(I32), 0)
        nc.sync.dma_start(two_list[:], two)
        nc.sync.dma_start(offs_list[:], offs)
        for quadrant in range(4):
            nc.sync.dma_start(
                table_scales[32 * quadrant : 32 * quadrant + 4, :].bitcast(I32),
                x_scales[0, 4 * quadrant : 4 * quadrant + 4, :].bitcast(I32),
            )
        nc.sync.dma_start(table_words[:].bitcast(I32), x_words[0].rearrange("p n s -> p (n s)").bitcast(I32))

        def load_weight(name, w):
            raw = sbuf(name, [P, PACK, w.shape[1]], F32)
            nc.sync.dma_start(raw[:], w.rearrange("(p s) c -> p s c", s=PACK))
            return raw

        w2_raw = load_weight("w2_raw", w2)
        w1_halves = [load_weight("w1_raw%d" % half, w1[:, half * H // 2 : (half + 1) * H // 2]) for half in range(2)]
        nc.sync.dma_start(nb_list[:], nb)
        gain = sbuf("gain", [P, PACK], F32)
        nc.sync.dma_start(gain[:], gn.rearrange("(p t) o -> p (t o)", t=PACK))
        w3_raw = load_weight("w3_raw", w3)
        res_rows = sbuf("res_rows", [P, ROW_BLOCKS, S], F32)
        nc.sync.dma_start(res_rows[:], res.rearrange("(b p) j -> p b j", p=P))

        identity = sbuf("identity", [P, P], F32)
        make_identity(nc, identity[:])
        minus_gain = sbuf("minus_gain", [P, PACK], F32)
        nc.vector.tensor_scalar_mul(minus_gain[:], gain[:], -1.0)

        def pick(name, table, entries, dtype):
            picked = sbuf(name, [P, S], dtype)
            nc.vector.tensor_copy(picked[:], table[:].indirect(entries[:]))
            return picked

        two_scales = pick("two_scales", table_scales, two_list, U8)
        offs_scales = pick("offs_scales", table_scales, offs_list, U8)
        two_words = pick("two_words", table_words, two_list, U32)
        offs_words = pick("offs_words", table_words, offs_list, U32)

        def round_and_deal(copy, target, source):
            copy(target.rearrange("p t m s -> p m t s"), source.rearrange("p s m t -> p m t s"))

        def quantize(name, values, width):
            words = sbuf(name + "_words", [P, width], U32)
            scales = sbuf(name + "_scales", [P, width], U8)
            nc.vector.quantize_mx(out=words[:].bitcast(FP8X4), scales=scales[:], in_=values)
            return words, scales

        def product(acc, weight, block, moving):
            cols = slice(block * P, (block + 1) * P)
            nc.tensor.matmul_mx(
                out=acc,
                lhsT=weight[0][:, cols].bitcast(FP8X4),
                lhsT_scale=weight[1][:, cols],
                rhs=moving[0][:].bitcast(FP8X4),
                rhs_scale=moving[1][:],
                start=True,
                stop=True,
            )

        w2_columns = w2_raw[:].rearrange("p s (m t) -> p s m t", t=PACK)
        w2_dealt = [sbuf("w2_dealt%d" % pair, [P, 2, P, PACK], BF16) for pair in range(2)]
        round_and_deal(nc.vector.tensor_copy, w2_dealt[0][:], w2_columns[:, :, :, :2])
        round_and_deal(nc.scalar.copy, w2_dealt[1][:], w2_columns[:, :, :, 2:])
        w1_dealt = sbuf("w1_dealt", [P, PACK, P, PACK], BF16)
        w1_columns = [raw[:].rearrange("p s (m t) -> p s m t", t=PACK) for raw in w1_halves]
        round_and_deal(nc.scalar.copy, w1_dealt[:, :, : P // 2, :], w1_columns[0])
        e = []
        for t in range(PACK):
            w2_mx = quantize("w2_%d" % t, w2_dealt[t // 2][:, t % 2].rearrange("p m s -> p (m s)"), P)
            acc = bank(t, [P, S])
            product(acc[:], w2_mx, 0, (two_words, two_scales))
            e.append(sbuf("e%d" % t, [P, S], F32))
            nc.scalar.activation(e[t][:], acc[:], ACT.Exp, scale=-1.0)

        round_and_deal(nc.vector.tensor_copy, w1_dealt[:, :, P // 2 :, :], w1_columns[1])
        w1_mx = quantize("w1", w1_dealt[:].rearrange("p t m s -> p (t m s)"), H)
        minus_y = []
        for t in range(PACK):
            acc = bank(4 + t, [P, S])
            product(acc[:], w1_mx, t, (offs_words, offs_scales))
            minus_y.append(sbuf("minus_y%d" % t, [P, S], F32))
            nc.scalar.activation(minus_y[t][:], acc[:], ACT.Copy, scale=minus_gain[:, t : t + 1])

        def neighbours(half):
            return nb_list[:, half * HALF // PER_COLUMN : (half + 1) * HALF // PER_COLUMN]

        def turn(acc, tiles, first_place, start, stop):
            for t in range(PACK):
                nc.tensor.matmul(
                    acc[:, t * P : (t + 1) * P],
                    tiles[t][:, first_place : first_place + QUARTER],
                    identity[:],
                    start=start and t == 0,
                    stop=stop and t == PACK - 1,
                    is_transpose=True,
                )

        e_sum = [bank(quarter, [P, H]) for quarter in range(4)]
        y_diff = [bank(4 + quarter, [P, H]) for quarter in range(4)]

        def open_sums(banks, tiles, half):
            for quarter in (2 * half, 2 * half + 1):
                turn(banks[quarter], tiles, quarter * QUARTER, True, False)

        def close_sums(banks, near, half):
            for u in range(2):
                turn(banks[2 * half + u], [near[:, t, :] for t in range(PACK)], u * QUARTER, False, True)

        def add_e_near(half, on_scalar):
            near = sbuf("e_near%d" % half, [P, PACK, HALF], F32)
            for t in range(PACK):
                if t < on_scalar:
                    nc.scalar.activation(near[:, t, :], e[t][:].indirect(neighbours(half)), ACT.Copy)
                else:
                    nc.vector.tensor_copy(near[:, t, :], e[t][:].indirect(neighbours(half)))
            close_sums(e_sum, near, half)

        def add_y_near(half):
            near = sbuf("y_near%d" % half, [P, PACK, HALF], F32)
            for t in range(PACK):
                looked_up = minus_y[t][:].indirect(neighbours(half))
                nc.vector.tensor_scalar(near[:, t, :], looked_up, -1.0, 0.0, ALU.mult, ALU.add)
            close_sums(y_diff, near, half)

        for half in range(2):
            open_sums(e_sum, e, half)
        add_e_near(0, 0)
        add_e_near(1, SCALAR_E_GATHERS)
        for half in range(2):
            open_sums(y_diff, minus_y, half)
        add_y_near(0)

        w3_rounded = sbuf("w3_rounded", [P, N, PACK], BF16)
        nc.vector.tensor_copy(
            w3_rounded[:].rearrange("p (c i) s -> p c s i", i=4),
            w3_raw[:].rearrange("p s (c i) -> p c s i", i=4),
        )
        w3_mx = quantize("w3", w3_rounded[:].rearrange("p c s -> p (c s)"), N)

        def in_pairs(acc):
            return acc[:].rearrange("j (u v p) -> j u p v", u=2, v=2)

        def factor(quarter):
            root = sbuf("factor%d" % quarter, [P, 2, P, 2], F32)
            nc.scalar.activation(root[:], in_pairs(e_sum[quarter]), ACT.Abs_reciprocal_sqrt, scale=0.25, bias=0.5)
            nc.scalar.activation(root[:], root[:], ACT.Square)
            return root

        def flux(quarter, root):
            turned = sbuf("z_turned%d" % quarter, [P, 2, P, 2], BF16)
            nc.vector.tensor_tensor(turned[:], in_pairs(y_diff[quarter]), root[:], ALU.mult)
            pairs = turned[:].rearrange("j u p v -> j (u p v)").bitcast(F32)
            back = bank(quarter, [P, 2, QUARTER])
            for u in range(2):
                nc.tensor.transpose(back[:, u, :], pairs[:, u * P : (u + 1) * P], identity[:])
            z = sbuf("z%d" % quarter, [P, QUARTER * PACK], BF16)
            nc.scalar.copy(z[:].bitcast(F32).rearrange("p (j u) -> p j u", u=2), back[:].rearrange("p u j -> p j u"))
            return z

        def layer(quarter, z):
            z_mx = quantize("z%d" % quarter, z[:], QUARTER)
            acc = bank(4 + quarter, [P, ROW_BLOCKS, QUARTER])
            for block in range(ROW_BLOCKS):
                product(acc[:, block, :], w3_mx, block, z_mx)
            return acc

        def finish(quarter, acc, pieces):
            places = slice(quarter * QUARTER, (quarter + 1) * QUARTER)
            rows = out[:, places].rearrange("(b p) j -> p b j", p=P)
            step = ROW_BLOCKS // pieces
            for first in range(0, ROW_BLOCKS, step):
                blocks = slice(first, first + step)
                result = sbuf("result%d_%d" % (quarter, first), [P, step, QUARTER], F32)
                nc.vector.tensor_tensor(result[:], acc[:, blocks, :], res_rows[:, blocks, places], ALU.add)
                nc.sync.dma_start(rows[:, blocks, :], result[:])

        roots = [factor(0), factor(1)]
        add_y_near(1)
        z, sums = [], []
        for step in range(6):
            if step < 2:
                roots.append(factor(step + 2))
            if step < 4:
                z.append(flux(step, roots[step]))
            if 1 <= step < 5:
                sums.append(layer(step - 1, z[step - 1]))
            if step >= 2:
                finish(step - 2, sums[step - 2], 2 if step == 5 else 1)
